import numpy as np
import ml_dtypes


def mxq(x, axis, fmt="e4m3"):
    dtype, down = {"e4m3": (ml_dtypes.float8_e4m3fn, 7), "e5m2": (ml_dtypes.float8_e5m2, 14)}[fmt]
    v = np.moveaxis(np.asarray(x, np.float32).astype(ml_dtypes.bfloat16).astype(np.float64), axis, -1)
    blocks = v.reshape(v.shape[:-1] + (-1, 32))
    amax = np.abs(blocks).max(-1, keepdims=True)
    byte = np.maximum(np.where(amax > 0, np.frexp(amax)[1] - 1 + 127, 0) - down, 1)
    scale = np.exp2(byte - 127.0)
    codes = (blocks / scale).astype(np.float32).astype(dtype).astype(np.float64)
    return np.moveaxis((codes * scale).reshape(v.shape), -1, axis)


WIDE = False


def mx_kscale(k):
    if not WIDE:
        return np.ones(k)
    levels = np.array([10, -10, 5, -5, 0])
    if k % 512:
        return np.exp2(np.random.permutation(np.resize(levels, k // 32))).repeat(32)
    a = np.empty((k // 512, 16))
    for p in range(k // 512):
        a[p, :8] = np.random.permutation(np.resize(levels, 8))
        for g in range(8):
            far = levels[np.abs(levels - a[p, g]) >= 10]
            a[p, g + 8] = far[np.random.randint(len(far))]
    return np.exp2(a.ravel()).repeat(32)


def f64(x):
    return np.asarray(x).astype(np.float64)


def striped(idx):
    return np.tile(idx.reshape(-1, 16).T, (8, 1)).astype(np.uint16)


def unstriped(offs):
    return offs[:16].T.reshape(-1).astype(np.int64)


E2M1 = np.array([0.0, 0.5, 1.0, 1.5, 2.0, 3.0, 4.0, 6.0, -0.0, -0.5, -1.0, -1.5, -2.0, -3.0, -4.0, -6.0])


def pack_weight(w, fmt):
    k, n = w.shape
    w = f64(np.asarray(w, np.float32).astype(ml_dtypes.bfloat16)).reshape(k // 32, 32, n)
    amax = np.abs(w).max(1)
    if fmt == "e4m3":
        byte = np.frexp(amax)[1] - 1 + 127 - 7
    else:
        mant, ex = np.frexp(amax / 6.0)
        byte = np.where(mant > 0.5, ex, ex - 1) + 127
    byte = np.clip(np.where(amax > 0, byte, 1), 1, 254)
    scaled = (w * np.exp2(127.0 - byte)[:, None, :]).reshape(k, n).astype(np.float32)
    by_word = np.ascontiguousarray(scaled.reshape(k // 512, 128, 4, n).transpose(0, 1, 3, 2))
    if fmt == "e4m3":
        words = by_word.astype(ml_dtypes.float8_e4m3fn).view(np.uint8)
    else:
        c = by_word.astype(ml_dtypes.float4_e2m1fn).view(np.uint8) & 0xF
        words = (c[..., 0::2] | (c[..., 1::2] << 4)).reshape(k // 512, 128, 2 * n)
    return np.ascontiguousarray(words), np.ascontiguousarray(byte.astype(np.uint8).reshape(k // 512, 16, n))


def unpack_weight(words, scales, fmt):
    g, _, n = scales.shape
    words = np.ascontiguousarray(words).reshape(g, 128, n, -1)
    if fmt == "e4m3":
        vals = words.view(ml_dtypes.float8_e4m3fn).astype(np.float64)
    else:
        nib = np.empty((g, 128, n, 4), np.uint8)
        nib[..., 0::2] = words & 0xF
        nib[..., 1::2] = words >> 4
        vals = E2M1[nib]
    vals = vals * np.repeat(np.exp2(scales.astype(np.float64) - 127.0), 8, axis=1)[..., None]
    return vals.transpose(0, 1, 3, 2).reshape(g * 512, n)


def gelu(v):
    return 0.5 * v * (1.0 + np.tanh(np.sqrt(2.0 / np.pi) * (v + 0.044715 * v**3)))


K, T, S, H, T2, P, N = 1024, 2048, 1024, 1024, 2048, 1024, 512

def setup_inputs():
    n = np.random.standard_normal
    s = mx_kscale(K)[:, None]
    u = mx_kscale(H)[:, None]
    tab_words, tab_scales = pack_weight(n((K, T)) * s, "e4m3")
    w1 = 0.8 * n((K, H)) / np.sqrt(K) / s
    w2_words, w2_scales = pack_weight(0.8 * n((K, H)) / np.sqrt(K) / s, "e2m1")
    w3 = n((H, N)) / np.sqrt(H) / u
    gain = np.random.choice([-1.0, 1.0], H) * np.random.uniform(1.0, 4.0, H) * u[:, 0]
    return {
        "tab_words": tab_words, "tab_scales": tab_scales,
        "offs": striped(np.random.permutation(T)[:S]),
        "offs2": striped(np.random.permutation(T2)[:S]),
        "offs3": striped(np.random.permutation(T2)[:P]),
        "w1": w1.astype(np.float32),
        "w2_words": w2_words, "w2_scales": w2_scales,
        "w3": w3.astype(np.float32),
        "page0": (0.8 * n((H, T2))).astype(np.float32),
        "wgs": np.exp(0.3 * n((128, S))).astype(np.float32),
        "slope": np.random.uniform(1, 3, H).astype(np.float32),
        "share": np.random.uniform(0.1, 0.5, H).astype(np.float32),
        "gain": gain.astype(np.float32),
    }

def reference(tab_words, tab_scales, offs, offs2, offs3, w1, w2_words, w2_scales, w3,
              page0, wgs, slope, share, gain):
    v = unpack_weight(tab_words, tab_scales, "e4m3")[:, unstriped(offs)]
    near = mxq(f64(w1), 0, "e4m3").T @ v
    far = unpack_weight(w2_words, w2_scales, "e2m1").T @ v
    h = np.maximum(near, far)
    page = f64(page0).copy()
    page[:, unstriped(offs2)] = np.tile(f64(wgs), (H // 128, 1)) * h
    top = page.max(axis=1)
    x = 1.0 / (1.0 + np.exp(-f64(slope)[:, None] * (page[:, unstriped(offs3)] - f64(share)[:, None] * top[:, None])))
    y = mxq(f64(gain)[:, None] * x, 0, "e4m3")
    return mxq(f64(w3), 0, "e4m3").T @ y

from contextlib import ExitStack

import concourse.mybir as mybir
from concourse.masks import make_identity

K, T, S, H, T2, LOOK, N = 1024, 2048, 1024, 1024, 2048, 1024, 512
FLOPS = 2 * (2 * K * H * S + H * N * LOOK)

F32 = mybir.dt.float32
BF16 = mybir.dt.bfloat16
I32 = mybir.dt.int32
U32 = mybir.dt.uint32
U16 = mybir.dt.uint16
U8 = mybir.dt.uint8
FP8X4 = mybir.dt.float8_e4m3fn_x4
FP4X4 = mybir.dt.float4_e2m1fn_x4
ACT = mybir.ActivationFunctionType
ALU = mybir.AluOpType
AXIS = mybir.AxisListType

P = 128
PACK = 4
K_PASS = P * PACK
BANK = 512
PASSES = K // K_PASS
R_PASSES = H // K_PASS
TILES = R_PASSES * PACK
HALVES = S // BANK
GROUPS = P // PACK


def tile_list_tenant_wing_corridors_kernel(
    tc, tab_words, tab_scales, offs, offs2, offs3, w1, w2_words, w2_scales, w3, page0, wgs, slope, share, gain, out
):
    nc = tc.nc

    def slot_rows(matrix, i):
        return matrix.rearrange("(g i e) c -> i g e c", i=PACK, e=PACK)[i]

    with ExitStack() as ctx:
        lists = ctx.enter_context(tc.tile_pool(name="lists", bufs=1))
        keep = ctx.enter_context(tc.tile_pool(name="keep", bufs=1))
        ring = ctx.enter_context(tc.tile_pool(name="ring", bufs=2))
        psum = ctx.enter_context(tc.psum_pool(name="psum", bufs=1))

        def bank(n, shape):
            return psum.tile(shape, F32, name="bank%d" % n)

        pick = lists.tile([P, S // 16], U16, name="pick")
        put = lists.tile([P, S // 16], U16, name="put")
        look = lists.tile([P, LOOK // 16], U16, name="look")

        tab_s = keep.tile([P, T], U8, name="tab_s", align_bytes=64)
        w2_s_raw = keep.tile([P, PASSES * H], U8, name="w2_s_raw", align_bytes=64)
        v_s = [keep.tile([P, S], U8, name="v_s%d" % a, align_bytes=64) for a in range(PASSES)]
        vec_rows = keep.tile([P, R_PASSES * P], F32, name="vec_rows")
        ident = keep.tile([P, P], F32, name="ident")
        nc.vector.memset(tab_s[:].bitcast(I32), 0)
        nc.vector.memset(w2_s_raw[:].bitcast(I32), 0)
        nc.vector.memset(v_s[1][:].bitcast(I32), 0)
        nc.vector.memset(vec_rows[:], 0.0)
        nc.vector.memset(ident[:], 0.0)
        make_identity(nc, ident[:], nomemset=True)

        def load_w1(a, b):
            raw = ring.tile([P, PACK, K_PASS], F32, name="raw", bufs=3)
            block = w1[a * K_PASS : (a + 1) * K_PASS, b * K_PASS : (b + 1) * K_PASS]
            nc.sync.dma_start(out=raw[:], in_=block.rearrange("(p j) c -> p j c", j=PACK))
            return raw

        def load_tab(a):
            words = keep.tile([P, T], U32, name="tab_w%d" % a, align_bytes=64)
            nc.sync.dma_start(
                out=words[:].bitcast(I32), in_=tab_words[a].rearrange("p t i -> p (t i)").bitcast(I32)
            )
            return words

        def load_w2(b):
            raw = keep.tile([P, PASSES, K_PASS // 2], U32, name="w2_raw%d" % b)
            words = w2_words.bitcast(I32).rearrange("a p c -> p a c")
            nc.sync.dma_start(
                out=raw[:].bitcast(I32), in_=words[:, :, b * K_PASS // 2 : (b + 1) * K_PASS // 2]
            )
            return raw

        def load_wgs(n):
            i, half = divmod(n, HALVES)
            tile = keep.tile([P, BANK], F32, name="wgs%d" % n, align_bytes=64)
            rows = slot_rows(wgs[:, half * BANK : (half + 1) * BANK], i)
            for q in range(4):
                nc.sync.dma_start(out=tile[32 * q : 32 * q + 32, :], in_=rows)
            return tile

        def load_page(t):
            b, i = divmod(t, PACK)
            page = ring.tile([P, T2], F32, name="page", bufs=4)
            nc.sync.dma_start(out=page[:], in_=slot_rows(page0[b * K_PASS : (b + 1) * K_PASS, :], i))
            return page

        def load_w3(b):
            raw = ring.tile([P, PACK, N], F32, name="raw", bufs=3)
            for i in range(PACK):
                nc.sync.dma_start(out=raw[:, i, :], in_=slot_rows(w3[b * K_PASS : (b + 1) * K_PASS, :], i))
            return raw

        nc.sync.dma_start(pick[:], offs)
        w2_raw = [load_w2(0)]
        for q in (0, 2, 1, 3):
            nc.sync.dma_start(
                out=tab_s[32 * q : 32 * q + 8, :].bitcast(I32), in_=tab_scales.bitcast(I32)[:, 4 * q : 4 * q + 4, :]
            )
        tab_w = [load_tab(0)]
        tab_w.append(load_tab(1))
        for q in (0, 2, 1, 3):
            nc.sync.dma_start(
                out=w2_s_raw[32 * q : 32 * q + 4, :].bitcast(I32).rearrange("r (a c) -> r a c", a=PASSES),
                in_=w2_scales.bitcast(I32).rearrange("a r c -> r a c")[4 * q : 4 * q + 4],
            )
        w1_raw = {(0, 0): load_w1(0, 0)}
        w1_raw[1, 0] = load_w1(1, 0)
        nc.sync.dma_start(put[:], offs2)
        wgs_sb = [load_wgs(0)]
        pages = [load_page(0)]
        wgs_sb.append(load_wgs(1))
        nc.sync.dma_start(look[:], offs3)
        for v, vec in enumerate((slope, share, gain)):
            nc.sync.dma_start(
                out=vec_rows[PACK * v : PACK * (v + 1), :].rearrange("i (g e) -> i g e", e=PACK),
                in_=vec.rearrange("(g i e) -> i g e", i=PACK, e=PACK),
            )
        w2_raw.append(load_w2(1))
        for a in range(PASSES):
            w1_raw[a, 1] = load_w1(a, 1)
        for t in range(1, PACK):
            wgs_sb.extend(load_wgs(HALVES * t + half) for half in range(HALVES))
            pages.append(load_page(t))
        w3_raw = [load_w3(b) for b in range(R_PASSES)]
        for t in range(PACK, TILES):
            pages.append(load_page(t))

        v_w = [keep.tile([P, S], U32, name="v_w%d" % a, align_bytes=64) for a in range(PASSES)]
        nc.vector.tensor_copy(v_s[0][:], tab_s[:].indirect(pick[:]))
        nc.scalar.dma_start(out=v_s[1][0:100, :].bitcast(I32), in_=v_s[0][4:104, :].bitcast(I32))
        for a in range(PASSES):
            nc.vector.tensor_copy(v_w[a][:], tab_w[a][:].indirect(pick[:]))

        par = keep.tile([P, R_PASSES * 3 * PACK], F32, name="par")
        coef = keep.tile([P, TILES], F32, name="coef")

        def row_parameters():
            turned = bank(6, [P, R_PASSES, P])
            for b in range(R_PASSES):
                nc.tensor.transpose(turned[:, b, :], vec_rows[:, b * P : (b + 1) * P], ident[:])
            nc.scalar.copy(par[:].rearrange("p (b c) -> p b c", b=R_PASSES), turned[:, :, 0 : 3 * PACK])
            par3 = par[:].rearrange("p (b v i) -> p v b i", b=R_PASSES, v=3)
            minus = keep.tile([P, R_PASSES, PACK], F32, name="minus")
            nc.gpsimd.tensor_scalar(minus[:], par3[:, 0], -1.0, 0.0, ALU.mult, ALU.add)
            nc.gpsimd.tensor_tensor(coef[:].rearrange("p (b i) -> p b i", b=R_PASSES), minus[:], par3[:, 1], ALU.mult)

        def par_column(v, t):
            b, i = divmod(t, PACK)
            c = (b * 3 + v) * PACK + i
            return par[:, c : c + 1]

        w2_s = keep.tile([P, PASSES * H], U8, name="w2_s", align_bytes=64)
        nc.scalar.copy(
            w2_s[:].bitcast(U32).rearrange("p (c i g) -> p c i g", i=PACK, g=GROUPS),
            w2_s_raw[:].bitcast(U32).rearrange("p (c g i) -> p c i g", i=PACK, g=GROUPS),
        )

        def deal_w2(b):
            dealt = keep.tile([P, PASSES * PACK * 2 * P], U8, name="w2_w%d" % b, align_bytes=64)
            nc.scalar.copy(
                dealt[:].bitcast(U32).rearrange("p (a i g w) -> p a i g w", a=PASSES, i=PACK, w=2),
                w2_raw[b][:].rearrange("p a (g i w) -> p a i g w", i=PACK, w=2),
            )
            return dealt

        def round_w1(copy, a, b, first, count):
            rounded = ring.tile([P, count * K_PASS], BF16, name="w1_bf%d" % count, bufs=2, align_bytes=64)
            copy(
                rounded[:].rearrange("p (i g e j) -> p i g e j", i=count, e=PACK, j=PACK),
                w1_raw[a, b][:].rearrange("p j (g i e) -> p i g e j", i=PACK, e=PACK)[:, first : first + count],
            )
            return rounded

        def quantise(codes, scales, rounded):
            nc.vector.quantize_mx(out=codes.bitcast(FP8X4), scales=scales, in_=rounded[:])

        w1_s = [keep.tile([P, PASSES * K_PASS], U8, name="w1_s%d" % b, align_bytes=64) for b in range(R_PASSES)]
        w1_w = [keep.tile([P, PASSES * K_PASS], U32, name="w1_w0", align_bytes=64)]
        w2_w = [deal_w2(0)]
        quantise(w1_w[0][:, :K_PASS], w1_s[0][:, :K_PASS], round_w1(nc.vector.tensor_copy, 0, 0, 0, PACK))
        for i in range(PACK):
            cols = slice(K_PASS + i * P, K_PASS + (i + 1) * P)
            quantise(w1_w[0][:, cols], w1_s[0][:, cols], round_w1(nc.vector.tensor_copy, 1, 0, i, 1))

        def readings(n):
            t, half = divmod(n, HALVES)
            b, i = divmod(t, PACK)
            cols = slice(half * BANK, (half + 1) * BANK)
            far = bank(4 + n % 2, [P, BANK])
            for a in range(PASSES):
                w0 = (a * PACK + i) * 2 * P
                s0 = ((a * R_PASSES + b) * PACK + i) * P
                nc.tensor.matmul_mx(
                    out=far[:],
                    lhsT=w2_w[b][:, w0 : w0 + 2 * P].bitcast(FP4X4),
                    lhsT_scale=w2_s[:, s0 : s0 + P],
                    rhs=v_w[a][:, cols].bitcast(FP8X4),
                    rhs_scale=v_s[a][:, cols],
                    start=(a == 0),
                    stop=(a == PASSES - 1),
                )
            near = bank(n % 4, [P, BANK])
            for a in range(PASSES):
                c0 = (a * PACK + i) * P
                nc.tensor.matmul_mx(
                    out=near[:],
                    lhsT=w1_w[b][:, c0 : c0 + P].bitcast(FP8X4),
                    lhsT_scale=w1_s[b][:, c0 : c0 + P],
                    rhs=v_w[a][:, cols].bitcast(FP8X4),
                    rhs_scale=v_s[a][:, cols],
                    start=(a == 0),
                    stop=(a == PASSES - 1),
                )
            far_sb = ring.tile([P, BANK], F32, name="far_sb", bufs=4)
            nc.scalar.copy(far_sb[:], far[:])
            return near, far_sb

        def join(n):
            near, far_sb = sums[n]
            if n == 3:
                h = keep.tile([P, BANK], F32, name="h3", align_bytes=64)
            else:
                h = ring.tile([P, BANK], F32, name="h", bufs=3)
            nc.vector.tensor_tensor(h[:], near[:], far_sb[:], ALU.max)
            return h

        top = keep.tile([P, TILES], F32, name="top")
        bias = keep.tile([P, TILES], F32, name="bias")
        y_bf = {
            (b, half): keep.tile([P, PACK * BANK], BF16, name="y_bf%d%d" % (b, half), align_bytes=64)
            for b in range(R_PASSES)
            for half in range(HALVES)
        }

        def change_page(n, h):
            t, half = divmod(n, HALVES)
            nc.vector.tensor_tensor(
                pages[t][:].indirect(put[:, half * 32 : (half + 1) * 32]),
                h[:],
                wgs_sb[n % (PACK * HALVES)][:],
                ALU.mult,
            )

        def gates(t):
            b, i = divmod(t, PACK)
            nc.scalar.activation(bias[:, t : t + 1], top[:, t : t + 1], ACT.Copy, scale=coef[:, t : t + 1])
            xs = []
            for half in range(HALVES):
                x = ring.tile([P, BANK], F32, name="x", bufs=4)
                nc.scalar.activation(
                    x[:],
                    pages[t][:].indirect(look[:, half * 32 : (half + 1) * 32]),
                    ACT.Sigmoid,
                    bias=bias[:, t : t + 1],
                    scale=par_column(0, t),
                )
                xs.append(x)
            return xs

        def y_slot(t, half):
            b, i = divmod(t, PACK)
            return y_bf[b, half][:].rearrange("p (m i) -> p i m", i=PACK)[:, i]

        def round_w3(b):
            rounded = keep.tile([P, PACK * N], BF16, name="w3_bf%d" % b, align_bytes=64)
            nc.scalar.copy(
                rounded[:].rearrange("p (n i) -> p n i", i=PACK), w3_raw[b][:].rearrange("p i n -> p n i")
            )
            return rounded

        y_s = [keep.tile([P, LOOK], U8, name="y_s%d" % b, align_bytes=64) for b in range(R_PASSES)]
        w3_s = keep.tile([P, R_PASSES * N], U8, name="w3_s", align_bytes=64)
        y_w = []
        w3_bf = []
        steps = TILES * HALVES
        sums = [readings(n) for n in range(4)]
        row_parameters()
        w2_w.append(deal_w2(1))
        w1_late = [round_w1(nc.scalar.copy, a, 1, 0, PACK) for a in range(PASSES)]
        hs = [join(n) for n in range(2)]
        for t in range(TILES):
            if t in (2, 3):
                w3_bf.append(round_w3(t - 2))
            for n in range(HALVES * t, HALVES * (t + 1)):
                change_page(n, hs[n])
                if n + 2 < steps:
                    hs.append(join(n + 2))
                if n + 4 < steps:
                    sums.append(readings(n + 4))
            nc.vector.reduce_max(top[:, t : t + 1], pages[t][:], AXIS.X)
            if t == 1:
                w1_w.append(keep.tile([P, PASSES * K_PASS], U32, name="w1_w1", tag="h3", align_bytes=64))
                for a in range(PASSES):
                    cols = slice(a * K_PASS, (a + 1) * K_PASS)
                    quantise(w1_w[1][:, cols], w1_s[1][:, cols], w1_late[a])
            xs = gates(t)
            if t < TILES - 1:
                for half in range(HALVES):
                    nc.scalar.activation(y_slot(t, half), xs[half][:], ACT.Copy, scale=par_column(2, t))
            if t == TILES - 2:
                y_w.append(keep.tile([P, LOOK], U32, name="y_w0", tag="wgs5", align_bytes=64))
                for half in range(HALVES):
                    cols = slice(half * BANK, (half + 1) * BANK)
                    quantise(y_w[0][:, cols], y_s[0][:, cols], y_bf[0, half])
        w3_w = keep.tile([P, R_PASSES * N], U32, name="w3_w", tag="wgs7", align_bytes=64)
        for b in range(R_PASSES):
            quantise(w3_w[:, b * N : (b + 1) * N], w3_s[:, b * N : (b + 1) * N], w3_bf[b])
        y_w.append(keep.tile([P, LOOK], U32, name="y_w1", align_bytes=64))

        def score(acc, b, half, nt):
            nc.tensor.matmul_mx(
                out=acc[:],
                lhsT=w3_w[:, b * N + nt * P : b * N + (nt + 1) * P].bitcast(FP8X4),
                lhsT_scale=w3_s[:, b * N + nt * P : b * N + (nt + 1) * P],
                rhs=y_w[b][:, half * BANK : (half + 1) * BANK].bitcast(FP8X4),
                rhs_scale=y_s[b][:, half * BANK : (half + 1) * BANK],
                start=(b == 0),
                stop=(b == R_PASSES - 1),
            )

        accs = {}
        for half in range(HALVES):
            for nt in range(N // P):
                accs[half, nt] = bank(half * 4 + nt, [P, BANK])
                score(accs[half, nt], 0, half, nt)
        for half in range(HALVES):
            nc.vector.tensor_scalar(
                y_slot(TILES - 1, half), xs[half][:], par_column(2, TILES - 1), None, ALU.mult
            )
            cols = slice(half * BANK, (half + 1) * BANK)
            quantise(y_w[1][:, cols], y_s[1][:, cols], y_bf[1, half])
            for nt in range(N // P):
                score(accs[half, nt], 1, half, nt)
                result = keep.tile([P, BANK], F32, name="result%d%d" % (half, nt))
                if half == 1 and nt % 2 == 0:
                    nc.vector.tensor_copy(result[:], accs[half, nt][:])
                else:
                    nc.scalar.copy(result[:], accs[half, nt][:])
                nc.sync.dma_start(out=out[nt * P : (nt + 1) * P, half * BANK : (half + 1) * BANK], in_=result[:])
